import numpy as np
import ml_dtypes


def mxq(x, axis, fmt="e4m3"):
    dtype, down = {"e4m3": (ml_dtypes.float8_e4m3fn, 7), "e5m2": (ml_dtypes.float8_e5m2, 14)}[fmt]
    v = np.moveaxis(np.asarray(x, np.float32).astype(ml_dtypes.bfloat16).astype(np.float64), axis, -1)
    blocks = v.reshape(v.shape[:-1] + (-1, 32))
    amax = np.abs(blocks).max(-1, keepdims=True)
    byte = np.maximum(np.where(amax > 0, np.frexp(amax)[1] - 1 + 127, 0) - down, 1)
    scale = np.exp2(byte - 127.0)
    codes = (blocks / scale).astype(np.float32).astype(dtype).astype(np.float64)
    return np.moveaxis((codes * scale).reshape(v.shape), -1, axis)


WIDE = False


def mx_kscale(k):
    if not WIDE:
        return np.ones(k)
    levels = np.array([10, -10, 5, -5, 0])
    if k % 512:
        return np.exp2(np.random.permutation(np.resize(levels, k // 32))).repeat(32)
    a = np.empty((k // 512, 16))
    for p in range(k // 512):
        a[p, :8] = np.random.permutation(np.resize(levels, 8))
        for g in range(8):
            far = levels[np.abs(levels - a[p, g]) >= 10]
            a[p, g + 8] = far[np.random.randint(len(far))]
    return np.exp2(a.ravel()).repeat(32)


def f64(x):
    return np.asarray(x).astype(np.float64)


def striped(idx):
    return np.tile(idx.reshape(-1, 16).T, (8, 1)).astype(np.uint16)


def unstriped(offs):
    return offs[:16].T.reshape(-1).astype(np.int64)


def pack_weight(w):
    k, n = w.shape
    w = f64(np.asarray(w, np.float32).astype(ml_dtypes.bfloat16)).reshape(k // 32, 32, n)
    amax = np.abs(w).max(1)
    byte = np.clip(np.where(amax > 0, np.frexp(amax)[1] - 1 + 127 - 7, 1), 1, 254)
    scaled = (w * np.exp2(127.0 - byte)[:, None, :]).reshape(k, n).astype(np.float32)
    words = np.ascontiguousarray(scaled.reshape(k // 512, 128, 4, n).transpose(0, 1, 3, 2)).astype(ml_dtypes.float8_e4m3fn).view(np.uint8)
    return words, np.ascontiguousarray(byte.astype(np.uint8).reshape(k // 512, 16, n))


def unpack_weight(words, scales):
    g, p, n, _ = words.shape
    vals = np.ascontiguousarray(words).view(ml_dtypes.float8_e4m3fn).astype(np.float64) * np.repeat(np.exp2(scales.astype(np.float64) - 127.0), 8, axis=1)[..., None]
    return vals.transpose(0, 1, 3, 2).reshape(g * 512, n)


def sigmoid(v):
    return 1.0 / (1.0 + np.exp(-np.maximum(v, -700.0)))


K, T, S, N = 1024, 2048, 512, 256


def setup_inputs():
    n = np.random.standard_normal
    s = mx_kscale(K)[:, None]
    packed_xT = pack_weight(n((K, T)) * s)
    return {
        "x_words": packed_xT[0],
        "x_scales": packed_xT[1],
        "w1": (n((K, N)) / np.sqrt(K) / s).astype(np.float32),
        "w2": (n((K, N)) / np.sqrt(K) / s).astype(np.float32),
        "pred": (n((N, S))).astype(np.float32),
        "offs": striped(np.random.permutation(T)[:S]),
    }


def reference(x_words, x_scales, w1, w2, pred, offs):
    xq = unpack_weight(x_words, x_scales)[:, unstriped(offs)]
    yf = mxq(f64(w1), 0, "e4m3").T @ xq
    yg = mxq(f64(w2), 0, "e4m3").T @ xq
    gain = 0.9 * sigmoid(yg)
    base0 = yf - (gain * (np.pad(f64(pred), ((0, 0), (0, 1)))[:, 1:]))
    base1 = base0 + gain * (np.pad(base0, ((0, 0), (0, 1)))[:, 1:])
    gg1 = gain * (np.pad(gain, ((0, 0), (0, 1)))[:, 1:])
    base2 = base1 + gg1 * (np.pad(base1, ((0, 0), (0, 2)))[:, 2:])
    gg2 = gg1 * (np.pad(gg1, ((0, 0), (0, 2)))[:, 2:])
    smo = base2 + gg2 * (np.pad(yf, ((0, 0), (0, 4)))[:, 4:])
    return ((smo - yf) ** 2) * np.sqrt(gain) + 0.3 * (np.abs(smo - (np.pad(smo, ((0, 0), (0, 1)))[:, 1:])))

@@ -1,0 +1,151 @@
+from contextlib import ExitStack
+
+import concourse.mybir as mybir
+
+K, T, S, N = 1024, 2048, 512, 256
+P = 128
+PACK = 4
+K_PASS = P * PACK
+PASSES = K // K_PASS
+TILES = N // P
+PAD = 8
+FLOPS = 2 * 2 * K * N * S
+
+F32 = mybir.dt.float32
+BF16 = mybir.dt.bfloat16
+I32 = mybir.dt.int32
+U32 = mybir.dt.uint32
+U16 = mybir.dt.uint16
+U8 = mybir.dt.uint8
+FP8X4 = mybir.dt.float8_e4m3fn_x4
+ALU = mybir.AluOpType
+ACT = mybir.ActivationFunctionType
+
+
+def tile_picked_yrts_jump_p_kernel(tc, x_words, x_scales, w1, w2, pred, offs, out):
+    nc = tc.nc
+    with ExitStack() as ctx:
+        keep = ctx.enter_context(tc.tile_pool(name="keep", bufs=1))
+        psum = ctx.enter_context(tc.psum_pool(name="psum", bufs=1))
+
+        offsets = keep.tile([P, S // 16], U16, name="offsets")
+        nc.sync.dma_start(offsets[:], offs)
+
+        warm = keep.tile([P, 2], F32, name="warm")
+        nc.vector.memset(warm[:, 0:1], 0.0)
+        warm_out = keep.tile([P, 1], F32, name="warm_out")
+        nc.scalar.activation(warm_out[:], warm[:, 0:1], ACT.Sigmoid)
+
+        table_scales = keep.tile([P, T], U8, name="table_scales", align_bytes=64)
+        nc.vector.memset(table_scales[:].bitcast(I32), 0)
+        for q in range(4):
+            nc.scalar.dma_start(
+                table_scales[32 * q : 32 * q + 4 * PASSES, :].bitcast(I32),
+                x_scales[:, 4 * q : 4 * q + 4, :].bitcast(I32),
+            )
+
+        table_words = []
+        for o in range(PASSES):
+            words = keep.tile([P, T], I32, name="table_words%d" % o, align_bytes=64)
+            nc.sync.dma_start(words[:], x_words[o].rearrange("p c r -> p (c r)").bitcast(I32))
+            table_words.append(words)
+
+        raw = {}
+        for name, w in (("g", w2), ("f", w1)):
+            for o in range(PASSES):
+                raw[name, o] = keep.tile([P, PACK, N], F32, name="raw_%s%d" % (name, o))
+                nc.sync.dma_start(
+                    raw[name, o][:], w[o * K_PASS : (o + 1) * K_PASS, :].rearrange("(p j) c -> p j c", j=PACK)
+                )
+        pred_sb = []
+        for t in range(TILES):
+            pt = keep.tile([P, S], F32, name="pred%d" % t)
+            nc.sync.dma_start(pt[:], pred[t * P : (t + 1) * P, :])
+            pred_sb.append(pt)
+
+        def padded(name):
+            tiles = []
+            for t in range(TILES):
+                tl = keep.tile([P, S + PAD], F32, name="%s%d" % (name, t))
+                nc.vector.memset(tl[:, S:], 0.0)
+                tiles.append(tl)
+            return tiles
+
+        def plain(name):
+            return [keep.tile([P, S], F32, name="%s%d" % (name, t)) for t in range(TILES)]
+
+        sig, d, h1, h3, smo = padded("sig"), padded("d"), padded("h1"), padded("h3"), padded("smo")
+        gg, root, t1, t2, corr = plain("gg"), plain("root"), plain("t1"), plain("t2"), plain("corr")
+        sq, jump, ajump, qq, res = plain("sq"), plain("jump"), plain("ajump"), plain("qq"), plain("res")
+
+        x_codes = []
+        for o in range(PASSES):
+            codes = keep.tile([P, S], U32, name="x_codes%d" % o, align_bytes=64)
+            nc.vector.tensor_copy(codes[:], table_words[o][:].bitcast(U32).indirect(offsets[:]))
+            x_codes.append(codes)
+            if o == 0:
+                x_plane = keep.tile([P, S], U8, name="x_plane", align_bytes=64)
+                nc.vector.tensor_copy(x_plane[:], table_scales[:].indirect(offsets[:]))
+
+        acc = {}
+        for name in ("g", "f"):
+            for t in range(TILES):
+                acc[name, t] = psum.tile([P, S], F32, name="acc_%s%d" % (name, t))
+            for o in range(PASSES):
+                grouped = []
+                for t in range(TILES):
+                    gr = keep.tile([P, P, PACK], BF16, name="grouped_%s%d%d" % (name, o, t), align_bytes=64)
+                    src = raw[name, o][:, :, t * P : (t + 1) * P].rearrange("p j (c i) -> p c j i", i=4)
+                    dst = gr[:].rearrange("p (c i) j -> p c j i", i=4)
+                    if t == 0:
+                        nc.vector.tensor_copy(dst, src)
+                    else:
+                        nc.scalar.copy(dst, src)
+                    grouped.append(gr)
+                for t in range(TILES):
+                    wc = keep.tile([P, P], U32, name="w_codes_%s%d%d" % (name, o, t), align_bytes=64)
+                    ws = keep.tile([P, P], U8, name="w_scales_%s%d%d" % (name, o, t), align_bytes=64)
+                    nc.vector.quantize_mx(
+                        out=wc[:].bitcast(FP8X4), scales=ws[:], in_=grouped[t][:].rearrange("p c j -> p (c j)")
+                    )
+                    nc.tensor.matmul_mx(
+                        out=acc[name, t][:],
+                        lhsT=wc[:].bitcast(FP8X4),
+                        lhsT_scale=ws[:],
+                        rhs=x_codes[o][:].bitcast(FP8X4),
+                        rhs_scale=x_plane[4 * o :, :],
+                        start=(o == 0),
+                        stop=(o == PASSES - 1),
+                    )
+            if name == "g":
+                for t in range(TILES):
+                    nc.scalar.activation(sig[t][:, :S], acc["g", t][:], ACT.Sigmoid)
+                for t in range(TILES):
+                    nc.vector.scalar_tensor_tensor(gg[t][:], sig[t][:, :S], 0.81, sig[t][:, 1 : S + 1], ALU.mult, ALU.mult)
+
+        tiles = range(TILES)
+        for t in tiles:
+            nc.scalar.activation(root[t][:], sig[t][:, :S], ACT.Sqrt, scale=0.9)
+        for t in tiles:
+            nc.vector.tensor_tensor(d[t][:, :S], acc["f", t][:], pred_sb[t][:], ALU.subtract)
+        for t in tiles:
+            nc.vector.scalar_tensor_tensor(t1[t][:], sig[t][:, :S], 0.9, d[t][:, 1 : S + 1], ALU.mult, ALU.mult)
+        for t in tiles:
+            nc.vector.tensor_tensor(h1[t][:, :S], t1[t][:], d[t][:, :S], ALU.add)
+        for t in tiles:
+            nc.vector.tensor_tensor(t2[t][:], gg[t][:], h1[t][:, 2 : S + 2], ALU.mult)
+        for t in tiles:
+            nc.vector.tensor_tensor(h3[t][:, :S], t2[t][:], h1[t][:, :S], ALU.add)
+        for t in tiles:
+            nc.vector.scalar_tensor_tensor(corr[t][:], sig[t][:, :S], 0.9, h3[t][:, 1 : S + 1], ALU.mult, ALU.mult)
+            nc.scalar.activation(sq[t][:], corr[t][:], ACT.Square)
+        for t in tiles:
+            nc.vector.tensor_tensor(smo[t][:, :S], acc["f", t][:], corr[t][:], ALU.add)
+        for t in tiles:
+            nc.vector.tensor_tensor(jump[t][:], smo[t][:, :S], smo[t][:, 1 : S + 1], ALU.subtract)
+            nc.scalar.activation(ajump[t][:], jump[t][:], ACT.Abs, scale=0.3)
+        for t in tiles:
+            nc.vector.tensor_tensor(qq[t][:], sq[t][:], root[t][:], ALU.mult)
+        for t in tiles:
+            nc.vector.tensor_tensor(res[t][:], qq[t][:], ajump[t][:], ALU.add)
+            nc.sync.dma_start(out[t * P : (t + 1) * P, :], res[t][:])

@@ -31,36 +31,37 @@ def tile_picked_yrts_jump_p_kernel(tc, x_words, x_scales, w1, w2, pred, offs, ou
         offsets = keep.tile([P, S // 16], U16, name="offsets")
         nc.sync.dma_start(offsets[:], offs)
 
-        warm = keep.tile([P, 2], F32, name="warm")
-        nc.vector.memset(warm[:, 0:1], 0.0)
-        warm_out = keep.tile([P, 1], F32, name="warm_out")
-        nc.scalar.activation(warm_out[:], warm[:, 0:1], ACT.Sigmoid)
+        warm = keep.tile([P, 1], F32, name="warm", tag="late_words", align_bytes=64)
+        nc.vector.memset(warm[:], 0.0)
+        warm_out = keep.tile([P, 1], F32, name="warm_out", tag="stage")
+        nc.scalar.activation(warm_out[:], warm[:], ACT.Sigmoid)
 
         table_scales = keep.tile([P, T], U8, name="table_scales", align_bytes=64)
         nc.vector.memset(table_scales[:].bitcast(I32), 0)
         for q in range(4):
-            nc.scalar.dma_start(
+            nc.sync.dma_start(
                 table_scales[32 * q : 32 * q + 4 * PASSES, :].bitcast(I32),
                 x_scales[:, 4 * q : 4 * q + 4, :].bitcast(I32),
             )
 
         table_words = []
         for o in range(PASSES):
-            words = keep.tile([P, T], I32, name="table_words%d" % o, align_bytes=64)
+            words = keep.tile([P, T], I32, name="table_words%d" % o, tag=("early_words", "late_words")[o], align_bytes=64)
             nc.sync.dma_start(words[:], x_words[o].rearrange("p c r -> p (c r)").bitcast(I32))
             table_words.append(words)
 
+        stage = keep.tile([P, 2 * PASSES + 1, PACK * N], F32, name="stage", tag="stage")
         raw = {}
-        for name, w in (("g", w2), ("f", w1)):
+        for m, (name, w) in enumerate((("g", w2), ("f", w1))):
             for o in range(PASSES):
-                raw[name, o] = keep.tile([P, PACK, N], F32, name="raw_%s%d" % (name, o))
+                raw[name, o] = stage[:, m * PASSES + o, :].rearrange("p (j c) -> p j c", j=PACK)
                 nc.sync.dma_start(
-                    raw[name, o][:], w[o * K_PASS : (o + 1) * K_PASS, :].rearrange("(p j) c -> p j c", j=PACK)
+                    raw[name, o], w[o * K_PASS : (o + 1) * K_PASS, :].rearrange("(p j) c -> p j c", j=PACK)
                 )
         pred_sb = []
         for t in range(TILES):
-            pt = keep.tile([P, S], F32, name="pred%d" % t)
-            nc.sync.dma_start(pt[:], pred[t * P : (t + 1) * P, :])
+            pt = stage[:, 2 * PASSES, t * S : (t + 1) * S]
+            nc.sync.dma_start(pt, pred[t * P : (t + 1) * P, :])
             pred_sb.append(pt)
 
         def padded(name):
@@ -75,7 +76,7 @@ def tile_picked_yrts_jump_p_kernel(tc, x_words, x_scales, w1, w2, pred, offs, ou
             return [keep.tile([P, S], F32, name="%s%d" % (name, t)) for t in range(TILES)]
 
         sig, d, h1, h3, smo = padded("sig"), padded("d"), padded("h1"), padded("h3"), padded("smo")
-        gg, root, t1, t2, corr = plain("gg"), plain("root"), plain("t1"), plain("t2"), plain("corr")
+        gg, t1, t2, corr = plain("gg"), plain("t1"), plain("t2"), plain("corr")
         sq, jump, ajump, qq, res = plain("sq"), plain("jump"), plain("ajump"), plain("qq"), plain("res")
 
         x_codes = []
@@ -94,7 +95,9 @@ def tile_picked_yrts_jump_p_kernel(tc, x_words, x_scales, w1, w2, pred, offs, ou
             for o in range(PASSES):
                 grouped = []
                 for t in range(TILES):
-                    gr = keep.tile([P, P, PACK], BF16, name="grouped_%s%d%d" % (name, o, t), align_bytes=64)
+                    gr = keep.tile(
+                        [P, P, PACK], BF16, name="grouped_%s%d%d" % (name, o, t), tag="grouped_%s%d%d" % (name, o, t), align_bytes=64
+                    )
                     src = raw[name, o][:, :, t * P : (t + 1) * P].rearrange("p j (c i) -> p c j i", i=4)
                     dst = gr[:].rearrange("p (c i) j -> p c j i", i=4)
                     if t == 0:
@@ -124,10 +127,14 @@ def tile_picked_yrts_jump_p_kernel(tc, x_words, x_scales, w1, w2, pred, offs, ou
                     nc.vector.scalar_tensor_tensor(gg[t][:], sig[t][:, :S], 0.81, sig[t][:, 1 : S + 1], ALU.mult, ALU.mult)
 
         tiles = range(TILES)
+        root = [
+            keep.tile([P, S], F32, name="root%d" % t, tag="grouped_f%d%d" % (PASSES - 1, 1 - t), align_bytes=64)
+            for t in tiles
+        ]
         for t in tiles:
             nc.scalar.activation(root[t][:], sig[t][:, :S], ACT.Sqrt, scale=0.9)
         for t in tiles:
-            nc.vector.tensor_tensor(d[t][:, :S], acc["f", t][:], pred_sb[t][:], ALU.subtract)
+            nc.vector.tensor_tensor(d[t][:, :S], acc["f", t][:], pred_sb[t], ALU.subtract)
         for t in tiles:
             nc.vector.scalar_tensor_tensor(t1[t][:], sig[t][:, :S], 0.9, d[t][:, 1 : S + 1], ALU.mult, ALU.mult)
         for t in tiles:
@@ -146,6 +153,8 @@ def tile_picked_yrts_jump_p_kernel(tc, x_words, x_scales, w1, w2, pred, offs, ou
             nc.scalar.activation(ajump[t][:], jump[t][:], ACT.Abs, scale=0.3)
         for t in tiles:
             nc.vector.tensor_tensor(qq[t][:], sq[t][:], root[t][:], ALU.mult)
-        for t in tiles:
-            nc.vector.tensor_tensor(res[t][:], qq[t][:], ajump[t][:], ALU.add)
-            nc.sync.dma_start(out[t * P : (t + 1) * P, :], res[t][:])
+            pieces = (slice(0, S),) if t < TILES - 1 else (slice(0, S // 2), slice(S // 2, S))
+            for i, cols in enumerate(pieces):
+                nc.vector.tensor_tensor(res[t][:, cols], qq[t][:, cols], ajump[t][:, cols], ALU.add)
+                queue = nc.scalar if len(pieces) - i == 2 else nc.sync
+                queue.dma_start(out[t * P : (t + 1) * P, cols], res[t][:, cols])

@@ -28,13 +28,14 @@ def tile_picked_yrts_jump_p_kernel(tc, x_words, x_scales, w1, w2, pred, offs, ou
         keep = ctx.enter_context(tc.tile_pool(name="keep", bufs=1))
         psum = ctx.enter_context(tc.psum_pool(name="psum", bufs=1))
 
+        def rows_of_pass(w, o):
+            return w[o * K_PASS : (o + 1) * K_PASS, :].rearrange("(p j) c -> p j c", j=PACK)
+
+        raw = {}
+        raw["g", 0] = keep.tile([P, PACK, N], F32, name="raw_g0")[:]
+        nc.sync.dma_start(raw["g", 0], rows_of_pass(w2, 0))
         offsets = keep.tile([P, S // 16], U16, name="offsets")
         nc.sync.dma_start(offsets[:], offs)
-
-        warm = keep.tile([P, 1], F32, name="warm", tag="late_words", align_bytes=64)
-        nc.vector.memset(warm[:], 0.0)
-        warm_out = keep.tile([P, 1], F32, name="warm_out", tag="stage")
-        nc.scalar.activation(warm_out[:], warm[:], ACT.Sigmoid)
 
         table_scales = keep.tile([P, T], U8, name="table_scales", align_bytes=64)
         nc.vector.memset(table_scales[:].bitcast(I32), 0)
@@ -44,49 +45,45 @@ def tile_picked_yrts_jump_p_kernel(tc, x_words, x_scales, w1, w2, pred, offs, ou
                 x_scales[:, 4 * q : 4 * q + 4, :].bitcast(I32),
             )
 
-        table_words = []
-        for o in range(PASSES):
-            words = keep.tile([P, T], I32, name="table_words%d" % o, tag=("early_words", "late_words")[o], align_bytes=64)
-            nc.sync.dma_start(words[:], x_words[o].rearrange("p c r -> p (c r)").bitcast(I32))
-            table_words.append(words)
+        names = ("sig", "d", "h1", "h3", "smo")
+        zeros = keep.tile([P, len(names) * TILES, PAD], F32, name="zeros", tag="words", align_bytes=64)
+        nc.vector.memset(zeros[:], 0.0)
+        wide = keep.tile([P, len(names) * TILES, S + PAD], F32, name="wide")
+        nc.vector.tensor_copy(wide[:, :, S:], zeros[:])
+        sig, d, h1, h3, smo = [[wide[:, n * TILES + t, :] for t in range(TILES)] for n in range(len(names))]
 
-        stage = keep.tile([P, 2 * PASSES + 1, PACK * N], F32, name="stage", tag="stage")
-        raw = {}
-        for m, (name, w) in enumerate((("g", w2), ("f", w1))):
-            for o in range(PASSES):
-                raw[name, o] = stage[:, m * PASSES + o, :].rearrange("p (j c) -> p j c", j=PACK)
-                nc.sync.dma_start(
-                    raw[name, o], w[o * K_PASS : (o + 1) * K_PASS, :].rearrange("(p j) c -> p j c", j=PACK)
-                )
+        warm = keep.tile([P, 1], F32, name="warm")
+        nc.vector.memset(warm[:], 0.0)
+        warm_out = keep.tile([P, 1], F32, name="warm_out", tag="stage")
+        nc.scalar.activation(warm_out[:], warm[:], ACT.Sigmoid)
+
+        table_words = keep.tile([P, PASSES, T], I32, name="table_words", tag="words", align_bytes=64)
+        for o in range(PASSES):
+            nc.sync.dma_start(table_words[:, o, :], x_words[o].rearrange("p c r -> p (c r)").bitcast(I32))
+
+        stage = keep.tile([P, 2 * PASSES, PACK * N], F32, name="stage", tag="stage")
+        for row, (name, w, o) in enumerate((("g", w2, 1), ("f", w1, 0), ("f", w1, 1))):
+            raw[name, o] = stage[:, row, :].rearrange("p (j c) -> p j c", j=PACK)
+            nc.sync.dma_start(raw[name, o], rows_of_pass(w, o))
         pred_sb = []
         for t in range(TILES):
-            pt = stage[:, 2 * PASSES, t * S : (t + 1) * S]
+            pt = stage[:, 2 * PASSES - 1, t * S : (t + 1) * S]
             nc.sync.dma_start(pt, pred[t * P : (t + 1) * P, :])
             pred_sb.append(pt)
-
-        def padded(name):
-            tiles = []
-            for t in range(TILES):
-                tl = keep.tile([P, S + PAD], F32, name="%s%d" % (name, t))
-                nc.vector.memset(tl[:, S:], 0.0)
-                tiles.append(tl)
-            return tiles
 
         def plain(name):
             return [keep.tile([P, S], F32, name="%s%d" % (name, t)) for t in range(TILES)]
 
-        sig, d, h1, h3, smo = padded("sig"), padded("d"), padded("h1"), padded("h3"), padded("smo")
         gg, t1, t2, corr = plain("gg"), plain("t1"), plain("t2"), plain("corr")
         sq, jump, ajump, qq, res = plain("sq"), plain("jump"), plain("ajump"), plain("qq"), plain("res")
 
+        x_plane = keep.tile([P, S], U8, name="x_plane", align_bytes=64)
+        nc.vector.tensor_copy(x_plane[:], table_scales[:].indirect(offsets[:]))
         x_codes = []
         for o in range(PASSES):
             codes = keep.tile([P, S], U32, name="x_codes%d" % o, align_bytes=64)
-            nc.vector.tensor_copy(codes[:], table_words[o][:].bitcast(U32).indirect(offsets[:]))
+            nc.vector.tensor_copy(codes[:], table_words[:, o, :].bitcast(U32).indirect(offsets[:]))
             x_codes.append(codes)
-            if o == 0:
-                x_plane = keep.tile([P, S], U8, name="x_plane", align_bytes=64)
-                nc.vector.tensor_copy(x_plane[:], table_scales[:].indirect(offsets[:]))
 
         acc = {}
         for name in ("g", "f"):
@@ -100,7 +97,7 @@ def tile_picked_yrts_jump_p_kernel(tc, x_words, x_scales, w1, w2, pred, offs, ou
                     )
                     src = raw[name, o][:, :, t * P : (t + 1) * P].rearrange("p j (c i) -> p c j i", i=4)
                     dst = gr[:].rearrange("p (c i) j -> p c j i", i=4)
-                    if t == 0:
+                    if t == 0 and (name, o) != ("g", 0):
                         nc.vector.tensor_copy(dst, src)
                     else:
                         nc.scalar.copy(dst, src)

from contextlib import ExitStack

import concourse.mybir as mybir

K, T, S, N = 1024, 2048, 512, 256
P = 128
PACK = 4
K_PASS = P * PACK
PASSES = K // K_PASS
TILES = N // P
PAD = 8
FLOPS = 2 * 2 * K * N * S

F32 = mybir.dt.float32
BF16 = mybir.dt.bfloat16
I32 = mybir.dt.int32
U32 = mybir.dt.uint32
U16 = mybir.dt.uint16
U8 = mybir.dt.uint8
FP8X4 = mybir.dt.float8_e4m3fn_x4
ALU = mybir.AluOpType
ACT = mybir.ActivationFunctionType


def tile_picked_yrts_jump_p_kernel(tc, x_words, x_scales, w1, w2, pred, offs, out):
    nc = tc.nc
    with ExitStack() as ctx:
        keep = ctx.enter_context(tc.tile_pool(name="keep", bufs=1))
        psum = ctx.enter_context(tc.psum_pool(name="psum", bufs=1))

        def rows_of_pass(w, o):
            return w[o * K_PASS : (o + 1) * K_PASS, :].rearrange("(p j) c -> p j c", j=PACK)

        raw = {}
        raw["g", 0] = keep.tile([P, PACK, N], F32, name="raw_g0")[:]
        nc.sync.dma_start(raw["g", 0], rows_of_pass(w2, 0))
        offsets = keep.tile([P, S // 16], U16, name="offsets")
        nc.sync.dma_start(offsets[:], offs)

        table_scales = keep.tile([P, T], U8, name="table_scales", align_bytes=64)
        nc.vector.memset(table_scales[:].bitcast(I32), 0)
        for q in range(4):
            nc.sync.dma_start(
                table_scales[32 * q : 32 * q + 4 * PASSES, :].bitcast(I32),
                x_scales[:, 4 * q : 4 * q + 4, :].bitcast(I32),
            )

        names = ("sig", "d", "h1", "h3", "smo")
        zeros = keep.tile([P, len(names) * TILES, PAD], F32, name="zeros", tag="words", align_bytes=64)
        nc.vector.memset(zeros[:], 0.0)
        wide = keep.tile([P, len(names) * TILES, S + PAD], F32, name="wide")
        nc.vector.tensor_copy(wide[:, :, S:], zeros[:])
        sig, d, h1, h3, smo = [[wide[:, n * TILES + t, :] for t in range(TILES)] for n in range(len(names))]

        warm = keep.tile([P, 1], F32, name="warm")
        nc.vector.memset(warm[:], 0.0)
        warm_out = keep.tile([P, 1], F32, name="warm_out", tag="stage")
        nc.scalar.activation(warm_out[:], warm[:], ACT.Sigmoid)

        table_words = keep.tile([P, PASSES, T], I32, name="table_words", tag="words", align_bytes=64)
        for o in range(PASSES):
            nc.sync.dma_start(table_words[:, o, :], x_words[o].rearrange("p c r -> p (c r)").bitcast(I32))

        stage = keep.tile([P, 2 * PASSES, PACK * N], F32, name="stage", tag="stage")
        for row, (name, w, o) in enumerate((("g", w2, 1), ("f", w1, 0), ("f", w1, 1))):
            raw[name, o] = stage[:, row, :].rearrange("p (j c) -> p j c", j=PACK)
            nc.sync.dma_start(raw[name, o], rows_of_pass(w, o))
        pred_sb = []
        for t in range(TILES):
            pt = stage[:, 2 * PASSES - 1, t * S : (t + 1) * S]
            nc.sync.dma_start(pt, pred[t * P : (t + 1) * P, :])
            pred_sb.append(pt)

        def plain(name):
            return [keep.tile([P, S], F32, name="%s%d" % (name, t)) for t in range(TILES)]

        gg, t1, t2, corr = plain("gg"), plain("t1"), plain("t2"), plain("corr")
        sq, jump, ajump, qq, res = plain("sq"), plain("jump"), plain("ajump"), plain("qq"), plain("res")

        x_plane = keep.tile([P, S], U8, name="x_plane", align_bytes=64)
        nc.vector.tensor_copy(x_plane[:], table_scales[:].indirect(offsets[:]))
        x_codes = []
        for o in range(PASSES):
            codes = keep.tile([P, S], U32, name="x_codes%d" % o, align_bytes=64)
            nc.vector.tensor_copy(codes[:], table_words[:, o, :].bitcast(U32).indirect(offsets[:]))
            x_codes.append(codes)

        acc = {}
        for name in ("g", "f"):
            for t in range(TILES):
                acc[name, t] = psum.tile([P, S], F32, name="acc_%s%d" % (name, t))
            for o in range(PASSES):
                grouped = []
                for t in range(TILES):
                    gr = keep.tile(
                        [P, P, PACK], BF16, name="grouped_%s%d%d" % (name, o, t), tag="grouped_%s%d%d" % (name, o, t), align_bytes=64
                    )
                    src = raw[name, o][:, :, t * P : (t + 1) * P].rearrange("p j (c i) -> p c j i", i=4)
                    dst = gr[:].rearrange("p (c i) j -> p c j i", i=4)
                    if t == 0 and (name, o) != ("g", 0):
                        nc.vector.tensor_copy(dst, src)
                    else:
                        nc.scalar.copy(dst, src)
                    grouped.append(gr)
                for t in range(TILES):
                    wc = keep.tile([P, P], U32, name="w_codes_%s%d%d" % (name, o, t), align_bytes=64)
                    ws = keep.tile([P, P], U8, name="w_scales_%s%d%d" % (name, o, t), align_bytes=64)
                    nc.vector.quantize_mx(
                        out=wc[:].bitcast(FP8X4), scales=ws[:], in_=grouped[t][:].rearrange("p c j -> p (c j)")
                    )
                    nc.tensor.matmul_mx(
                        out=acc[name, t][:],
                        lhsT=wc[:].bitcast(FP8X4),
                        lhsT_scale=ws[:],
                        rhs=x_codes[o][:].bitcast(FP8X4),
                        rhs_scale=x_plane[4 * o :, :],
                        start=(o == 0),
                        stop=(o == PASSES - 1),
                    )
            if name == "g":
                for t in range(TILES):
                    nc.scalar.activation(sig[t][:, :S], acc["g", t][:], ACT.Sigmoid)
                for t in range(TILES):
                    nc.vector.scalar_tensor_tensor(gg[t][:], sig[t][:, :S], 0.81, sig[t][:, 1 : S + 1], ALU.mult, ALU.mult)

        tiles = range(TILES)
        root = [
            keep.tile([P, S], F32, name="root%d" % t, tag="grouped_f%d%d" % (PASSES - 1, 1 - t), align_bytes=64)
            for t in tiles
        ]
        for t in tiles:
            nc.scalar.activation(root[t][:], sig[t][:, :S], ACT.Sqrt, scale=0.9)
        for t in tiles:
            nc.vector.tensor_tensor(d[t][:, :S], acc["f", t][:], pred_sb[t], ALU.subtract)
        for t in tiles:
            nc.vector.scalar_tensor_tensor(t1[t][:], sig[t][:, :S], 0.9, d[t][:, 1 : S + 1], ALU.mult, ALU.mult)
        for t in tiles:
            nc.vector.tensor_tensor(h1[t][:, :S], t1[t][:], d[t][:, :S], ALU.add)
        for t in tiles:
            nc.vector.tensor_tensor(t2[t][:], gg[t][:], h1[t][:, 2 : S + 2], ALU.mult)
        for t in tiles:
            nc.vector.tensor_tensor(h3[t][:, :S], t2[t][:], h1[t][:, :S], ALU.add)
        for t in tiles:
            nc.vector.scalar_tensor_tensor(corr[t][:], sig[t][:, :S], 0.9, h3[t][:, 1 : S + 1], ALU.mult, ALU.mult)
            nc.scalar.activation(sq[t][:], corr[t][:], ACT.Square)
        for t in tiles:
            nc.vector.tensor_tensor(smo[t][:, :S], acc["f", t][:], corr[t][:], ALU.add)
        for t in tiles:
            nc.vector.tensor_tensor(jump[t][:], smo[t][:, :S], smo[t][:, 1 : S + 1], ALU.subtract)
            nc.scalar.activation(ajump[t][:], jump[t][:], ACT.Abs, scale=0.3)
        for t in tiles:
            nc.vector.tensor_tensor(qq[t][:], sq[t][:], root[t][:], ALU.mult)
            pieces = (slice(0, S),) if t < TILES - 1 else (slice(0, S // 2), slice(S // 2, S))
            for i, cols in enumerate(pieces):
                nc.vector.tensor_tensor(res[t][:, cols], qq[t][:, cols], ajump[t][:, cols], ALU.add)
                queue = nc.scalar if len(pieces) - i == 2 else nc.sync
                queue.dma_start(out[t * P : (t + 1) * P, cols], res[t][:, cols])
